import numpy as np
import ml_dtypes


def mxq(x, axis, fmt="e4m3"):
    dtype, down = {"e4m3": (ml_dtypes.float8_e4m3fn, 7), "e5m2": (ml_dtypes.float8_e5m2, 14)}[fmt]
    v = np.moveaxis(np.asarray(x, np.float32).astype(ml_dtypes.bfloat16).astype(np.float64), axis, -1)
    blocks = v.reshape(v.shape[:-1] + (-1, 32))
    amax = np.abs(blocks).max(-1, keepdims=True)
    byte = np.maximum(np.where(amax > 0, np.frexp(amax)[1] - 1 + 127, 0) - down, 1)
    scale = np.exp2(byte - 127.0)
    codes = (blocks / scale).astype(np.float32).astype(dtype).astype(np.float64)
    return np.moveaxis((codes * scale).reshape(v.shape), -1, axis)


WIDE = False


def mx_kscale(k):
    if not WIDE:
        return np.ones(k)
    levels = np.array([10, -10, 5, -5, 0])
    if k % 512:
        return np.exp2(np.random.permutation(np.resize(levels, k // 32))).repeat(32)
    a = np.empty((k // 512, 16))
    for p in range(k // 512):
        a[p, :8] = np.random.permutation(np.resize(levels, 8))
        for g in range(8):
            far = levels[np.abs(levels - a[p, g]) >= 10]
            a[p, g + 8] = far[np.random.randint(len(far))]
    return np.exp2(a.ravel()).repeat(32)


BF16 = ml_dtypes.bfloat16


def bf(x):
    return np.asarray(x, np.float32).astype(BF16)


def f64(x):
    return np.asarray(x).astype(np.float64)


N, D, K = 8192, 512, 256


def scale_rows(gain, m):
    return gain[:, None] * m


def draw0():
    s = mx_kscale(D)
    u = mx_kscale(N)
    return {
        "x": bf(np.random.standard_normal((N, D)) * s),
        "p": bf(np.random.standard_normal((D, D)) / np.sqrt(D) / s[:, None]),
        "beta": bf(np.random.standard_normal((D, K)) / np.sqrt(D) / s[:, None]),
        "r": bf(np.random.uniform(0.5, 1.5, N) * u),
        "t": bf((1.0 + 0.3 * np.random.standard_normal(N)) / u),
        "v": bf(np.random.standard_normal((D, K)) / np.sqrt(D)),
        "psi": bf(np.random.uniform(0.05, 0.2, D)),
    }


def core(x, p, beta, r, t, v, psi):
    n_cases = x.shape[0]
    xq = mxq(f64(x), 1, "e4m3")
    e0 = xq @ mxq(f64(p), 0, "e4m3")
    e = scale_rows(f64(r), e0)
    z0 = xq @ mxq(f64(beta), 0, "e4m3")
    z = scale_rows(f64(t), z0)
    c = mxq(e, 0, "e4m3").T @ mxq(z, 0, "e4m3")
    return (c / n_cases - f64(v)) / f64(psi)[:, None]


def e4m3fn_bytes(y):
    return np.clip(np.asarray(y, np.float64), -448.0, 448.0).astype(np.float32).astype(ml_dtypes.float8_e4m3fn).view(np.uint8)


def e4m3fn_values(b):
    return np.asarray(b, np.uint8).view(ml_dtypes.float8_e4m3fn).astype(np.float64)


def setup_inputs():
    d = draw0()
    x0 = np.asarray(d['x']).astype(np.float64)
    s = (np.max(np.abs(x0), axis=(0,), keepdims=True) / 448.0).astype(np.float32)
    out = {}
    for k, v in d.items():
        if k == 'x':
            out['x_bytes'] = e4m3fn_bytes(x0 / s.astype(np.float64))
            out['x_scale'] = s
        else:
            out[k] = v
    return out


def reference(x_bytes, x_scale, p, beta, r, t, v, psi):
    return core(e4m3fn_values(x_bytes) * x_scale.astype(np.float64), p, beta, r, t, v, psi)

@@ -1,0 +1,240 @@
+from contextlib import ExitStack
+
+import concourse.mybir as mybir
+from concourse.masks import make_identity
+
+N, D, K = 8192, 512, 256
+P = 128
+J = 4
+GROUP = P * J
+GROUPS = N // GROUP
+FLOPS = 2 * N * D * (D + K) + 2 * N * D * K
+
+F32 = mybir.dt.float32
+BF16 = mybir.dt.bfloat16
+U32 = mybir.dt.uint32
+U8 = mybir.dt.uint8
+FP8 = mybir.dt.float8_e4m3fn
+FP8X4 = mybir.dt.float8_e4m3fn_x4
+MULT = mybir.AluOpType.mult
+ADD = mybir.AluOpType.add
+SUB = mybir.AluOpType.subtract
+COPY = mybir.ActivationFunctionType.Copy
+
+CHUNKS = [("z", 0), ("z", 128), ("e", 0), ("e", 128), ("e", 256), ("e", 384)]
+
+
+def tile_factoranalysisemloadinggradient_t_kernel(tc, x_bytes, x_scale, p, beta, r, t, v, psi, out):
+    nc = tc.nc
+    with ExitStack() as ctx:
+        keep = ctx.enter_context(tc.tile_pool(name="keep", bufs=1))
+        work = ctx.enter_context(tc.tile_pool(name="work", bufs=2))
+        psum = ctx.enter_context(tc.psum_pool(name="psum", bufs=1))
+        ctx.enter_context(tc.manual_schedule())
+
+        xb = {}
+        xw = {}
+        xwords = {}
+        xp = {}
+        xi = {}
+        xc = {}
+        banks = {}
+        zi = {}
+        ei = {}
+        zq = {}
+        eq = {}
+
+        xv = x_bytes.rearrange("(g m j) k -> g m (j k)", m=P, j=J)
+
+        def load(g):
+            xb[g] = keep.tile([P, J * D], U8, name=f"x_bytes_{g}", align_bytes=64)
+            nc.sync.dma_start(out=xb[g][:], in_=xv[g])
+
+        rows = keep.tile([P, GROUP], BF16, name="rows", align_bytes=64)
+        nc.vector.memset(rows[:], 0.0)
+        psi_rows = keep.tile([P, P], BF16, name="psi_rows", align_bytes=64)
+        nc.vector.memset(psi_rows[:], 0.0)
+        dummy = keep.tile([P, 2], F32, name="dummy")
+        nc.vector.memset(dummy[:], 0.0)
+        nc.scalar.activation(out=dummy[:, 1:2], in_=dummy[:, 0:1], func=COPY)
+
+        load(0)
+        beta_raw = keep.tile([P, J, K], BF16, name="beta_raw", align_bytes=64)
+        nc.sync.dma_start(out=beta_raw[:], in_=beta.rearrange("(p t) n -> p t n", t=J))
+        p_raw = keep.tile([P, J, D], BF16, name="p_raw", align_bytes=64)
+        nc.sync.dma_start(out=p_raw[:], in_=p.rearrange("(p t) n -> p t n", t=J))
+        xs = keep.tile([P, J], F32, name="xs", align_bytes=64)
+        nc.scalar.dma_start(out=xs[:], in_=x_scale.rearrange("o (p t) -> p (o t)", t=J))
+        nc.scalar.dma_start(out=rows[0:GROUPS, :], in_=r.rearrange("(g q) -> g q", q=GROUP))
+        nc.scalar.dma_start(out=rows[GROUPS:2 * GROUPS, :], in_=t.rearrange("(g q) -> g q", q=GROUP))
+        nc.scalar.dma_start(out=psi_rows[0:J, :], in_=psi.rearrange("(j p) -> j p", p=P))
+        for g in range(1, 4):
+            load(g)
+        v_sb = keep.tile([P, J, K], BF16, name="v_sb", align_bytes=64)
+        nc.sync.dma_start(out=v_sb[:], in_=v.rearrange("(j p) n -> p j n", p=P))
+        for g in range(4, GROUPS):
+            load(g)
+
+        ident_f = keep.tile([P, P], F32, name="ident_f", align_bytes=64)
+        make_identity(nc, ident_f[:])
+        ident_b = keep.tile([P, P], BF16, name="ident_b", align_bytes=64)
+        nc.vector.tensor_copy(out=ident_b[:], in_=ident_f[:])
+
+        def cast(g, on_vector=0):
+            xw[g] = work.tile([P, J * D], BF16, name="xw", tag="xw", bufs=3, align_bytes=64)
+            half = J * D // 2
+            for h in range(2):
+                cols = slice(h * half, (h + 1) * half)
+                src = xb[g][:, cols].bitcast(FP8)
+                if h >= 2 - on_vector:
+                    nc.vector.tensor_copy(out=xw[g][:, cols], in_=src)
+                else:
+                    nc.scalar.copy(out=xw[g][:, cols], in_=src)
+
+        def transp(g, by_half=False):
+            words = xw[g][:].bitcast(F32)
+            b = [psum.tile([P, 512], F32, name=f"xwords{u}", tag=f"xwords{u}", bufs=1) for u in range(2)]
+            xwords[g] = b
+            order = [(u, j) for j in range(J) for u in range(2)] if by_half else [(u, j) for u in range(2) for j in range(J)]
+            for u, j in order:
+                src = words[:, 256 * j + u:256 * (j + 1):2]
+                if by_half:
+                    dst = b[j // 2][:, 256 * u + 128 * (j % 2):256 * u + 128 * (j % 2) + 128]
+                else:
+                    dst = b[u][:, 128 * j:128 * (j + 1)]
+                nc.tensor.transpose(dst, src, ident_f[:])
+
+        def new_xi(g):
+            xi[g] = work.tile([P, GROUP, J], BF16, name="xi", tag="xi", bufs=1, align_bytes=64)
+
+        def vexit(g):
+            new_xi(g)
+            for h in range(2):
+                src = xwords[g][h][:].bitcast(BF16).rearrange("p (u n e) -> p n u e", u=2, e=2)
+                dst = xi[g][:, 256 * h:256 * (h + 1), :].rearrange("p n (u e) -> p n u e", e=2)
+                sc = xs[:].rearrange("p (u e) -> p u e", e=2).unsqueeze(1).to_broadcast([P, 256, 2, 2])
+                nc.vector.tensor_tensor(out=dst, in0=src, in1=sc, op=MULT)
+
+        def sexit(g):
+            xp[g] = work.tile([P, J, GROUP], BF16, name="xp", tag="xp", bufs=2, align_bytes=64)
+            for tt in range(J):
+                src = xwords[g][tt // 2][:].bitcast(BF16).rearrange("p (n e) -> p e n", e=2)[:, tt % 2, :]
+                nc.scalar.activation(out=xp[g][:, tt, :], in_=src, func=COPY, scale=xs[:, tt:tt + 1])
+
+        def gil(g):
+            new_xi(g)
+            for h in range(2):
+                cols = slice(256 * h, 256 * (h + 1))
+                nc.gpsimd.tensor_scalar(
+                    out=xi[g][:, cols, :], in0=xp[g][:, :, cols].rearrange("p t n -> p n t"),
+                    scalar1=1.0, scalar2=0.0, op0=MULT, op1=ADD)
+
+        def quant(src, width, tag, bufs):
+            codes = work.tile([P, width], U32, name=tag + "c", tag=tag + "c", bufs=bufs, align_bytes=64)
+            scales = work.tile([P, width], U8, name=tag + "s", tag=tag + "s", bufs=bufs, align_bytes=64)
+            nc.vector.quantize_mx(out=codes[:].bitcast(FP8X4), scales=scales[:], in_=src.rearrange("p n j -> p (n j)"))
+            return codes, scales
+
+        def mm(i, ci):
+            kind, col = CHUNKS[ci]
+            bank = psum.tile([P, 512], F32, name="ez", tag="ez", bufs=4)
+            banks[i, ci] = bank
+            wc, wsc = (beta_q if kind == "z" else p_q)
+            for j in range(J):
+                nc.tensor.matmul_mx(
+                    out=bank[:, P * j:P * (j + 1)],
+                    lhsT=xc[i][0][:, P * j:P * (j + 1)].bitcast(FP8X4), lhsT_scale=xc[i][1][:, P * j:P * (j + 1)],
+                    rhs=wc[:, col:col + P].bitcast(FP8X4), rhs_scale=wsc[:, col:col + P],
+                    start=True, stop=True)
+
+        def drain(i, ci):
+            kind, col = CHUNKS[ci]
+            if ci == 0:
+                zi[i] = work.tile([P, K, J], BF16, name="zi", tag="zi", bufs=2, align_bytes=64)
+                ei[i] = work.tile([P, D, J], BF16, name="ei", tag="ei", bufs=2, align_bytes=64)
+            dst = (zi[i] if kind == "z" else ei[i])[:, col:col + P, :]
+            f = rt[:, (GROUPS + i if kind == "z" else i), :].unsqueeze(1).to_broadcast([P, P, J])
+            nc.vector.tensor_tensor(out=dst, in0=banks[i, ci][:].rearrange("p (j n) -> p n j", j=J), in1=f, op=MULT)
+
+        def st2(i):
+            for h in range(2):
+                nc.tensor.matmul_mx(
+                    out=acc[h][:],
+                    lhsT=zq[i][0][:, P * h:P * (h + 1)].bitcast(FP8X4), lhsT_scale=zq[i][1][:, P * h:P * (h + 1)],
+                    rhs=eq[i][0][:].bitcast(FP8X4), rhs_scale=eq[i][1][:],
+                    start=(i == 0), stop=(i == GROUPS - 1))
+
+        acc = [psum.tile([P, 512], F32, name=f"acc{h}", tag=f"acc{h}", bufs=1) for h in range(2)]
+
+        cast(0, on_vector=1)
+        cast(1)
+        rtp = psum.tile([P, 5, P], BF16, name="rtp", tag="ez", bufs=4)
+        for j in range(J):
+            nc.tensor.transpose(rtp[:, j, :], rows[:, j:GROUP:J], ident_b[:])
+        nc.tensor.transpose(rtp[:, 4, :], psi_rows[:], ident_b[:])
+        transp(0, by_half=True)
+
+        beta_i = keep.tile([P, K, J], BF16, name="beta_i", align_bytes=64)
+        nc.vector.tensor_copy(out=beta_i[:], in_=beta_raw[:].rearrange("p t n -> p n t"))
+        p_i = keep.tile([P, D, J], BF16, name="p_i", align_bytes=64)
+        for h in range(4):
+            cols = slice(P * h, P * (h + 1))
+            nc.gpsimd.tensor_scalar(out=p_i[:, cols, :], in0=p_raw[:, :, cols].rearrange("p t n -> p n t"),
+                                    scalar1=1.0, scalar2=0.0, op0=MULT, op1=ADD)
+        rt = keep.tile([P, 2 * GROUPS, J], F32, name="rt", align_bytes=64)
+        nc.vector.tensor_copy(out=rt[:], in_=rtp[:, 0:4, 0:2 * GROUPS].rearrange("p j c -> p c j"))
+        psi_c = keep.tile([P, J], F32, name="psi_c", align_bytes=64)
+        nc.vector.tensor_copy(out=psi_c[:], in_=rtp[:, 4, 0:J])
+        vexit(0)
+        beta_q = quant(beta_i[:], K, "beta", 1)
+        transp(1)
+        sexit(1)
+        cast(2)
+        xc[0] = quant(xi[0][:], GROUP, "x", 3)
+        inv = keep.tile([P, J], F32, name="inv", align_bytes=64)
+        nc.vector.reciprocal(out=inv[:], in_=psi_c[:])
+        p_q = quant(p_i[:], D, "p", 1)
+        inv_n = keep.tile([P, J], F32, name="inv_n", align_bytes=64)
+        nc.vector.tensor_scalar(out=inv_n[:], in0=inv[:], scalar1=1.0 / N, scalar2=None, op0=MULT)
+
+        mm(0, 0)
+        mm(0, 1)
+
+        vp = keep.tile([P, J, K], F32, name="vp", align_bytes=64)
+
+        for i in range(GROUPS):
+            if i > 0:
+                st2(i - 1)
+            if i + 1 < GROUPS:
+                gil(i + 1)
+            drain(i, 0)
+            drain(i, 1)
+            for ci in range(2, 6):
+                mm(i, ci)
+                drain(i, ci)
+            if i + 2 < GROUPS:
+                transp(i + 2)
+                sexit(i + 2)
+            if i + 3 < GROUPS:
+                cast(i + 3)
+            zq[i] = quant(zi[i][:], K, "z", 2)
+            if i + 1 < GROUPS:
+                xc[i + 1] = quant(xi[i + 1][:], GROUP, "x", 3)
+                mm(i + 1, 0)
+                mm(i + 1, 1)
+            eq[i] = quant(ei[i][:], D, "e", 2)
+            if i == GROUPS - 2:
+                for j in range(J):
+                    nc.gpsimd.tensor_scalar(out=vp[:, j, :], in0=v_sb[:, j, :], scalar1=inv[:, j:j + 1], scalar2=0.0, op0=MULT, op1=ADD)
+        st2(GROUPS - 1)
+
+        ct = keep.tile([P, 2, D], F32, name="ct", align_bytes=64)
+        nc.vector.tensor_copy(out=ct[:, 0, :], in_=acc[0][:])
+        nc.scalar.copy(out=ct[:, 1, :], in_=acc[1][:])
+        res = keep.tile([P, J, K], F32, name="res", align_bytes=64)
+        for j in range(J):
+            ob = psum.tile([P, K], F32, name="ob", tag="ez", bufs=4)
+            for h in range(2):
+                nc.tensor.transpose(ob[:, P * h:P * (h + 1)], ct[:, h, P * j:P * (j + 1)], ident_f[:])
+            nc.vector.scalar_tensor_tensor(out=res[:, j, :], in0=ob[:], scalar=inv_n[:, j:j + 1], in1=vp[:, j, :], op0=MULT, op1=SUB)
+            nc.sync.dma_start(out=out[P * j:P * (j + 1), :], in_=res[:, j, :])

@@ -21,6 +21,7 @@ ADD = mybir.AluOpType.add
 SUB = mybir.AluOpType.subtract
 COPY = mybir.ActivationFunctionType.Copy
 
+Z_ON_SCALAR = (13, 14, 15)
 CHUNKS = [("z", 0), ("z", 128), ("e", 0), ("e", 128), ("e", 256), ("e", 384)]
 
 
@@ -42,6 +43,7 @@ def tile_factoranalysisemloadinggradient_t_kernel(tc, x_bytes, x_scale, p, beta,
         zi = {}
         ei = {}
         zq = {}
+        zplanes = {}
         eq = {}
 
         xv = x_bytes.rearrange("(g m j) k -> g m (j k)", m=P, j=J)
@@ -59,16 +61,17 @@ def tile_factoranalysisemloadinggradient_t_kernel(tc, x_bytes, x_scale, p, beta,
         nc.scalar.activation(out=dummy[:, 1:2], in_=dummy[:, 0:1], func=COPY)
 
         load(0)
+        xs = keep.tile([P, J], F32, name="xs", align_bytes=64)
+        nc.sync.dma_start(out=xs[:], in_=x_scale.rearrange("o (p t) -> p (o t)", t=J))
+        load(1)
         beta_raw = keep.tile([P, J, K], BF16, name="beta_raw", align_bytes=64)
         nc.sync.dma_start(out=beta_raw[:], in_=beta.rearrange("(p t) n -> p t n", t=J))
         p_raw = keep.tile([P, J, D], BF16, name="p_raw", align_bytes=64)
         nc.sync.dma_start(out=p_raw[:], in_=p.rearrange("(p t) n -> p t n", t=J))
-        xs = keep.tile([P, J], F32, name="xs", align_bytes=64)
-        nc.scalar.dma_start(out=xs[:], in_=x_scale.rearrange("o (p t) -> p (o t)", t=J))
         nc.scalar.dma_start(out=rows[0:GROUPS, :], in_=r.rearrange("(g q) -> g q", q=GROUP))
         nc.scalar.dma_start(out=rows[GROUPS:2 * GROUPS, :], in_=t.rearrange("(g q) -> g q", q=GROUP))
         nc.scalar.dma_start(out=psi_rows[0:J, :], in_=psi.rearrange("(j p) -> j p", p=P))
-        for g in range(1, 4):
+        for g in range(2, 4):
             load(g)
         v_sb = keep.tile([P, J, K], BF16, name="v_sb", align_bytes=64)
         nc.sync.dma_start(out=v_sb[:], in_=v.rearrange("(j p) n -> p j n", p=P))
@@ -80,22 +83,23 @@ def tile_factoranalysisemloadinggradient_t_kernel(tc, x_bytes, x_scale, p, beta,
         ident_b = keep.tile([P, P], BF16, name="ident_b", align_bytes=64)
         nc.vector.tensor_copy(out=ident_b[:], in_=ident_f[:])
 
-        def cast(g, on_vector=0):
-            xw[g] = work.tile([P, J * D], BF16, name="xw", tag="xw", bufs=3, align_bytes=64)
+        def cast(g, h, eng=None):
+            if h == 0:
+                xw[g] = work.tile([P, J * D], BF16, name="xw", tag="xw", bufs=3, align_bytes=64)
             half = J * D // 2
-            for h in range(2):
-                cols = slice(h * half, (h + 1) * half)
-                src = xb[g][:, cols].bitcast(FP8)
-                if h >= 2 - on_vector:
-                    nc.vector.tensor_copy(out=xw[g][:, cols], in_=src)
-                else:
-                    nc.scalar.copy(out=xw[g][:, cols], in_=src)
+            cols = slice(h * half, (h + 1) * half)
+            src = xb[g][:, cols].bitcast(FP8)
+            if eng == "v":
+                nc.vector.tensor_copy(out=xw[g][:, cols], in_=src)
+            else:
+                nc.scalar.copy(out=xw[g][:, cols], in_=src)
 
-        def transp(g, by_half=False):
+        def transp(g, by_half=False, us=(0, 1)):
             words = xw[g][:].bitcast(F32)
-            b = [psum.tile([P, 512], F32, name=f"xwords{u}", tag=f"xwords{u}", bufs=1) for u in range(2)]
-            xwords[g] = b
-            order = [(u, j) for j in range(J) for u in range(2)] if by_half else [(u, j) for u in range(2) for j in range(J)]
+            b = xwords.setdefault(g, {})
+            for u in us:
+                b[u] = psum.tile([P, 512], F32, name=f"xwords{u}", tag="ez" if by_half else f"xwords{u}", bufs=4 if by_half else 1)
+            order = [(u, j) for j in range(J) for u in us] if by_half else [(u, j) for u in us for j in range(J)]
             for u, j in order:
                 src = words[:, 256 * j + u:256 * (j + 1):2]
                 if by_half:
@@ -115,16 +119,17 @@ def tile_factoranalysisemloadinggradient_t_kernel(tc, x_bytes, x_scale, p, beta,
                 sc = xs[:].rearrange("p (u e) -> p u e", e=2).unsqueeze(1).to_broadcast([P, 256, 2, 2])
                 nc.vector.tensor_tensor(out=dst, in0=src, in1=sc, op=MULT)
 
-        def sexit(g):
-            xp[g] = work.tile([P, J, GROUP], BF16, name="xp", tag="xp", bufs=2, align_bytes=64)
-            for tt in range(J):
+        def sexit(g, ts=(0, 1, 2, 3)):
+            if 0 in ts:
+                xp[g] = work.tile([P, J, GROUP], BF16, name="xp", tag="xp", bufs=2, align_bytes=64)
+            for tt in ts:
                 src = xwords[g][tt // 2][:].bitcast(BF16).rearrange("p (n e) -> p e n", e=2)[:, tt % 2, :]
                 nc.scalar.activation(out=xp[g][:, tt, :], in_=src, func=COPY, scale=xs[:, tt:tt + 1])
 
         def gil(g):
             new_xi(g)
-            for h in range(2):
-                cols = slice(256 * h, 256 * (h + 1))
+            for h in range(4):
+                cols = slice(P * h, P * (h + 1))
                 nc.gpsimd.tensor_scalar(
                     out=xi[g][:, cols, :], in0=xp[g][:, :, cols].rearrange("p t n -> p n t"),
                     scalar1=1.0, scalar2=0.0, op0=MULT, op1=ADD)
@@ -139,6 +144,14 @@ def tile_factoranalysisemloadinggradient_t_kernel(tc, x_bytes, x_scale, p, beta,
             kind, col = CHUNKS[ci]
             bank = psum.tile([P, 512], F32, name="ez", tag="ez", bufs=4)
             banks[i, ci] = bank
+            if kind == "z" and i in Z_ON_SCALAR:
+                for jj in range(2):
+                    j = 2 * ci + jj
+                    nc.tensor.matmul_mx(
+                        out=bank[:, K * jj:K * (jj + 1)],
+                        lhsT=xc[i][0][:, P * j:P * (j + 1)].bitcast(FP8X4), lhsT_scale=xc[i][1][:, P * j:P * (j + 1)],
+                        rhs=beta_q[0][:].bitcast(FP8X4), rhs_scale=beta_q[1][:], start=True, stop=True)
+                return
             wc, wsc = (beta_q if kind == "z" else p_q)
             for j in range(J):
                 nc.tensor.matmul_mx(
@@ -154,7 +167,17 @@ def tile_factoranalysisemloadinggradient_t_kernel(tc, x_bytes, x_scale, p, beta,
                 ei[i] = work.tile([P, D, J], BF16, name="ei", tag="ei", bufs=2, align_bytes=64)
             dst = (zi[i] if kind == "z" else ei[i])[:, col:col + P, :]
             f = rt[:, (GROUPS + i if kind == "z" else i), :].unsqueeze(1).to_broadcast([P, P, J])
-            nc.vector.tensor_tensor(out=dst, in0=banks[i, ci][:].rearrange("p (j n) -> p n j", j=J), in1=f, op=MULT)
+            src = banks[i, ci][:].rearrange("p (j n) -> p n j", j=J)
+            if kind == "z" and i in Z_ON_SCALAR:
+                if ci == 0:
+                    zplanes[i] = work.tile([P, J, K], BF16, name="zplanes", tag="zplanes", bufs=2, align_bytes=64)
+                for jj in range(2):
+                    j = 2 * ci + jj
+                    nc.scalar.activation(out=zplanes[i][:, j, :], in_=banks[i, ci][:, K * jj:K * (jj + 1)], func=COPY, scale=rt[:, GROUPS + i, j:j + 1])
+                if ci == 1:
+                    nc.scalar.copy(out=zi[i][:], in_=zplanes[i][:].rearrange("p j n -> p n j"))
+            else:
+                nc.vector.tensor_tensor(out=dst, in0=f, in1=src, op=MULT)
 
         def st2(i):
             for h in range(2):
@@ -166,13 +189,18 @@ def tile_factoranalysisemloadinggradient_t_kernel(tc, x_bytes, x_scale, p, beta,
 
         acc = [psum.tile([P, 512], F32, name=f"acc{h}", tag=f"acc{h}", bufs=1) for h in range(2)]
 
-        cast(0, on_vector=1)
-        cast(1)
+        cast(0, 0)
+        cast(0, 1, "v")
+        cast(1, 0, "v")
+        cast(1, 1, "v")
+        cast(2, 0)
+        cast(2, 1)
+        transp(0, by_half=True)
+        transp(1)
         rtp = psum.tile([P, 5, P], BF16, name="rtp", tag="ez", bufs=4)
         for j in range(J):
             nc.tensor.transpose(rtp[:, j, :], rows[:, j:GROUP:J], ident_b[:])
         nc.tensor.transpose(rtp[:, 4, :], psi_rows[:], ident_b[:])
-        transp(0, by_half=True)
 
         beta_i = keep.tile([P, K, J], BF16, name="beta_i", align_bytes=64)
         nc.vector.tensor_copy(out=beta_i[:], in_=beta_raw[:].rearrange("p t n -> p n t"))
@@ -181,15 +209,14 @@ def tile_factoranalysisemloadinggradient_t_kernel(tc, x_bytes, x_scale, p, beta,
             cols = slice(P * h, P * (h + 1))
             nc.gpsimd.tensor_scalar(out=p_i[:, cols, :], in0=p_raw[:, :, cols].rearrange("p t n -> p n t"),
                                     scalar1=1.0, scalar2=0.0, op0=MULT, op1=ADD)
+        vexit(0)
         rt = keep.tile([P, 2 * GROUPS, J], F32, name="rt", align_bytes=64)
         nc.vector.tensor_copy(out=rt[:], in_=rtp[:, 0:4, 0:2 * GROUPS].rearrange("p j c -> p c j"))
         psi_c = keep.tile([P, J], F32, name="psi_c", align_bytes=64)
         nc.vector.tensor_copy(out=psi_c[:], in_=rtp[:, 4, 0:J])
-        vexit(0)
         beta_q = quant(beta_i[:], K, "beta", 1)
-        transp(1)
         sexit(1)
-        cast(2)
+        cast(3, 0)
         xc[0] = quant(xi[0][:], GROUP, "x", 3)
         inv = keep.tile([P, J], F32, name="inv", align_bytes=64)
         nc.vector.reciprocal(out=inv[:], in_=psi_c[:])
@@ -197,31 +224,38 @@ def tile_factoranalysisemloadinggradient_t_kernel(tc, x_bytes, x_scale, p, beta,
         inv_n = keep.tile([P, J], F32, name="inv_n", align_bytes=64)
         nc.vector.tensor_scalar(out=inv_n[:], in0=inv[:], scalar1=1.0 / N, scalar2=None, op0=MULT)
 
-        mm(0, 0)
-        mm(0, 1)
-
         vp = keep.tile([P, J, K], F32, name="vp", align_bytes=64)
+        for ci in range(4):
+            mm(0, ci)
 
         for i in range(GROUPS):
-            if i > 0:
-                st2(i - 1)
             if i + 1 < GROUPS:
                 gil(i + 1)
             drain(i, 0)
             drain(i, 1)
-            for ci in range(2, 6):
-                mm(i, ci)
-                drain(i, ci)
+            drain(i, 2)
+            drain(i, 3)
             if i + 2 < GROUPS:
-                transp(i + 2)
-                sexit(i + 2)
-            if i + 3 < GROUPS:
-                cast(i + 3)
+                transp(i + 2, us=(0,))
+            mm(i, 4)
+            mm(i, 5)
+            if i + 2 < GROUPS:
+                sexit(i + 2, (0, 1))
+                if i + 3 < GROUPS:
+                    cast(i + 3, 1)
+                transp(i + 2, us=(1,))
+                sexit(i + 2, (2, 3))
+                if i + 4 < GROUPS:
+                    cast(i + 4, 0)
+            drain(i, 4)
+            drain(i, 5)
+            if i > 0:
+                st2(i - 1)
             zq[i] = quant(zi[i][:], K, "z", 2)
             if i + 1 < GROUPS:
                 xc[i + 1] = quant(xi[i + 1][:], GROUP, "x", 3)
-                mm(i + 1, 0)
-                mm(i + 1, 1)
+                for ci in range(4):
+                    mm(i + 1, ci)
             eq[i] = quant(ei[i][:], D, "e", 2)
             if i == GROUPS - 2:
                 for j in range(J):

@@ -21,7 +21,10 @@ ADD = mybir.AluOpType.add
 SUB = mybir.AluOpType.subtract
 COPY = mybir.ActivationFunctionType.Copy
 
-Z_ON_SCALAR = (13, 14, 15)
+Z_ON_SCALAR = (14, 15)
+GIL_S = ()
+SEQ = "g0 g1 gs d0 d1 d2 d3 T0 m4 m5 T1 s01 s23 c3b c4a d4 d5 st2 qxa qxb qz M0 M1 M2 M3 qe vp".split()
+SEQ_OF = {0: "g0 g1 gs d0 d1 d2 d3 m4 m5 T0 s01 T1 s23 c3b c4a d4 d5 st2 qxa qxb qz M0 M1 M2 M3 qe vp".split()}
 CHUNKS = [("z", 0), ("z", 128), ("e", 0), ("e", 128), ("e", 256), ("e", 384)]
 
 
@@ -83,7 +86,10 @@ def tile_factoranalysisemloadinggradient_t_kernel(tc, x_bytes, x_scale, p, beta,
         ident_b = keep.tile([P, P], BF16, name="ident_b", align_bytes=64)
         nc.vector.tensor_copy(out=ident_b[:], in_=ident_f[:])
 
+        done = set()
+
         def cast(g, h, eng=None):
+            done.add((g, h))
             if h == 0:
                 xw[g] = work.tile([P, J * D], BF16, name="xw", tag="xw", bufs=3, align_bytes=64)
             half = J * D // 2
@@ -128,8 +134,8 @@ def tile_factoranalysisemloadinggradient_t_kernel(tc, x_bytes, x_scale, p, beta,
 
         def gil(g):
             new_xi(g)
-            for h in range(4):
-                cols = slice(P * h, P * (h + 1))
+            for h in range(2):
+                cols = slice(256 * h, 256 * (h + 1))
                 nc.gpsimd.tensor_scalar(
                     out=xi[g][:, cols, :], in0=xp[g][:, :, cols].rearrange("p t n -> p n t"),
                     scalar1=1.0, scalar2=0.0, op0=MULT, op1=ADD)
@@ -139,6 +145,14 @@ def tile_factoranalysisemloadinggradient_t_kernel(tc, x_bytes, x_scale, p, beta,
             scales = work.tile([P, width], U8, name=tag + "s", tag=tag + "s", bufs=bufs, align_bytes=64)
             nc.vector.quantize_mx(out=codes[:].bitcast(FP8X4), scales=scales[:], in_=src.rearrange("p n j -> p (n j)"))
             return codes, scales
+
+        def qx(g, h):
+            if h == 0:
+                xc[g] = (work.tile([P, GROUP], U32, name="xcodes", tag="xcodes", bufs=3, align_bytes=64),
+                         work.tile([P, GROUP], U8, name="xscales", tag="xscales", bufs=3, align_bytes=64))
+            cols = slice(256 * h, 256 * (h + 1))
+            nc.vector.quantize_mx(out=xc[g][0][:, cols].bitcast(FP8X4), scales=xc[g][1][:, cols],
+                                  in_=xi[g][:, cols, :].rearrange("p n j -> p (n j)"))
 
         def mm(i, ci):
             kind, col = CHUNKS[ci]
@@ -189,12 +203,10 @@ def tile_factoranalysisemloadinggradient_t_kernel(tc, x_bytes, x_scale, p, beta,
 
         acc = [psum.tile([P, 512], F32, name=f"acc{h}", tag=f"acc{h}", bufs=1) for h in range(2)]
 
-        cast(0, 0)
-        cast(0, 1, "v")
+        cast(0, 0, "v")
+        cast(0, 1)
         cast(1, 0, "v")
         cast(1, 1, "v")
-        cast(2, 0)
-        cast(2, 1)
         transp(0, by_half=True)
         transp(1)
         rtp = psum.tile([P, 5, P], BF16, name="rtp", tag="ez", bufs=4)
@@ -203,24 +215,30 @@ def tile_factoranalysisemloadinggradient_t_kernel(tc, x_bytes, x_scale, p, beta,
         nc.tensor.transpose(rtp[:, 4, :], psi_rows[:], ident_b[:])
 
         beta_i = keep.tile([P, K, J], BF16, name="beta_i", align_bytes=64)
-        nc.vector.tensor_copy(out=beta_i[:], in_=beta_raw[:].rearrange("p t n -> p n t"))
+        nc.scalar.copy(out=beta_i[:], in_=beta_raw[:].rearrange("p t n -> p n t"))
         p_i = keep.tile([P, D, J], BF16, name="p_i", align_bytes=64)
         for h in range(4):
             cols = slice(P * h, P * (h + 1))
-            nc.gpsimd.tensor_scalar(out=p_i[:, cols, :], in0=p_raw[:, :, cols].rearrange("p t n -> p n t"),
-                                    scalar1=1.0, scalar2=0.0, op0=MULT, op1=ADD)
+            src = p_raw[:, :, cols].rearrange("p t n -> p n t")
+            if h < 2:
+                nc.scalar.copy(out=p_i[:, cols, :], in_=src)
+            else:
+                nc.gpsimd.tensor_scalar(out=p_i[:, cols, :], in0=src, scalar1=1.0, scalar2=0.0, op0=MULT, op1=ADD)
         vexit(0)
         rt = keep.tile([P, 2 * GROUPS, J], F32, name="rt", align_bytes=64)
         nc.vector.tensor_copy(out=rt[:], in_=rtp[:, 0:4, 0:2 * GROUPS].rearrange("p j c -> p c j"))
         psi_c = keep.tile([P, J], F32, name="psi_c", align_bytes=64)
         nc.vector.tensor_copy(out=psi_c[:], in_=rtp[:, 4, 0:J])
+        qx(0, 0)
         beta_q = quant(beta_i[:], K, "beta", 1)
         sexit(1)
+        cast(2, 0)
+        cast(2, 1)
         cast(3, 0)
-        xc[0] = quant(xi[0][:], GROUP, "x", 3)
         inv = keep.tile([P, J], F32, name="inv", align_bytes=64)
         nc.vector.reciprocal(out=inv[:], in_=psi_c[:])
         p_q = quant(p_i[:], D, "p", 1)
+        qx(0, 1)
         inv_n = keep.tile([P, J], F32, name="inv_n", align_bytes=64)
         nc.vector.tensor_scalar(out=inv_n[:], in0=inv[:], scalar1=1.0 / N, scalar2=None, op0=MULT)
 
@@ -228,38 +246,68 @@ def tile_factoranalysisemloadinggradient_t_kernel(tc, x_bytes, x_scale, p, beta,
         for ci in range(4):
             mm(0, ci)
 
+        def gil_half(g, h, eng):
+            if h == 0:
+                new_xi(g)
+            cols = slice(256 * h, 256 * (h + 1))
+            src = xp[g][:, :, cols].rearrange("p t n -> p n t")
+            if eng == "s":
+                nc.scalar.copy(out=xi[g][:, cols, :], in_=src)
+            else:
+                nc.gpsimd.tensor_scalar(out=xi[g][:, cols, :], in0=src, scalar1=1.0, scalar2=0.0, op0=MULT, op1=ADD)
+
+        def do(i, tok):
+            if tok == "g0":
+                if i + 1 < GROUPS:
+                    gil_half(i + 1, 0, "g")
+            elif tok == "g1":
+                if i + 1 < GROUPS and i + 1 not in GIL_S:
+                    gil_half(i + 1, 1, "g")
+            elif tok == "gs":
+                if i + 1 < GROUPS and i + 1 in GIL_S:
+                    gil_half(i + 1, 1, "s")
+            elif tok[0] == "d":
+                drain(i, int(tok[1]))
+            elif tok[0] == "m":
+                mm(i, int(tok[1]))
+            elif tok[0] == "M":
+                if i + 1 < GROUPS:
+                    mm(i + 1, int(tok[1]))
+            elif tok[0] == "T":
+                if i + 2 < GROUPS:
+                    transp(i + 2, us=(int(tok[1]),))
+            elif tok == "s01":
+                if i + 2 < GROUPS:
+                    sexit(i + 2, (0, 1))
+            elif tok == "s23":
+                if i + 2 < GROUPS:
+                    sexit(i + 2, (2, 3))
+            elif tok[0] == "c":
+                g = i + int(tok[1])
+                h = 0 if tok[2] == "a" else 1
+                if g < GROUPS and (g, h) not in done:
+                    cast(g, h)
+            elif tok == "st2":
+                if i > 0:
+                    st2(i - 1)
+            elif tok == "qxa":
+                if i + 1 < GROUPS:
+                    qx(i + 1, 0)
+            elif tok == "qxb":
+                if i + 1 < GROUPS:
+                    qx(i + 1, 1)
+            elif tok == "qz":
+                zq[i] = quant(zi[i][:], K, "z", 2)
+            elif tok == "qe":
+                eq[i] = quant(ei[i][:], D, "e", 2)
+            elif tok == "vp":
+                if i == GROUPS - 3:
+                    for j in range(J):
+                        nc.scalar.activation(out=vp[:, j, :], in_=v_sb[:, j, :], func=COPY, scale=inv[:, j:j + 1])
+
         for i in range(GROUPS):
-            if i + 1 < GROUPS:
-                gil(i + 1)
-            drain(i, 0)
-            drain(i, 1)
-            drain(i, 2)
-            drain(i, 3)
-            if i + 2 < GROUPS:
-                transp(i + 2, us=(0,))
-            mm(i, 4)
-            mm(i, 5)
-            if i + 2 < GROUPS:
-                sexit(i + 2, (0, 1))
-                if i + 3 < GROUPS:
-                    cast(i + 3, 1)
-                transp(i + 2, us=(1,))
-                sexit(i + 2, (2, 3))
-                if i + 4 < GROUPS:
-                    cast(i + 4, 0)
-            drain(i, 4)
-            drain(i, 5)
-            if i > 0:
-                st2(i - 1)
-            zq[i] = quant(zi[i][:], K, "z", 2)
-            if i + 1 < GROUPS:
-                xc[i + 1] = quant(xi[i + 1][:], GROUP, "x", 3)
-                for ci in range(4):
-                    mm(i + 1, ci)
-            eq[i] = quant(ei[i][:], D, "e", 2)
-            if i == GROUPS - 2:
-                for j in range(J):
-                    nc.gpsimd.tensor_scalar(out=vp[:, j, :], in0=v_sb[:, j, :], scalar1=inv[:, j:j + 1], scalar2=0.0, op0=MULT, op1=ADD)
+            for tok in SEQ_OF.get(i, SEQ):
+                do(i, tok)
         st2(GROUPS - 1)
 
         ct = keep.tile([P, 2, D], F32, name="ct", align_bytes=64)

@@ -21,10 +21,11 @@ ADD = mybir.AluOpType.add
 SUB = mybir.AluOpType.subtract
 COPY = mybir.ActivationFunctionType.Copy
 
-Z_ON_SCALAR = (14, 15)
+Z_ON_SCALAR = (15,)
+DIRECT_FROM = 13
 GIL_S = ()
-SEQ = "g0 g1 gs d0 d1 d2 d3 T0 m4 m5 T1 s01 s23 c3b c4a d4 d5 st2 qxa qxb qz M0 M1 M2 M3 qe vp".split()
-SEQ_OF = {0: "g0 g1 gs d0 d1 d2 d3 m4 m5 T0 s01 T1 s23 c3b c4a d4 d5 st2 qxa qxb qz M0 M1 M2 M3 qe vp".split()}
+SEQ = "g0 g1 gs d0 d1 d2 d3 T0 m4 m5 T1 s01 s23 c3b c4a vp d4 d5 st2 qxa qxb qz M0 M1 M2 M3 qe".split()
+SEQ_OF = {0: "g0 g1 gs d0 d1 d2 d3 m4 m5 T0 s01 T1 s23 c3b c4a d4 d5 st2 qxa qxb qz M0 M1 M2 M3 qe".split(), 1: "g0 g1 gs d0 d1 d2 d3 m4 m5 T0 s01 T1 s23 c3b c4a d4 d5 st2 qxa qxb qz M0 M1 M2 M3 qe".split(), 13: "g0 g1 gs d0 d1 d2 d3 T0 m4 m5 T1 s01 s23 c3b c4a d4 d5 st2 kt qxa qxb qz M0 M1 M2 M3 qe".split(), 14: "g0 g1 d0 d1 d2 d3 m4 m5 wt ws d4 d5 qxa qxb qz M0 M1 M2 M3 qe wg".split(), 15: "d0 d1 d2 d3 m4 m5 st2p st2 d4 d5 qz qe".split()}
 CHUNKS = [("z", 0), ("z", 128), ("e", 0), ("e", 128), ("e", 256), ("e", 384)]
 
 
@@ -63,7 +64,10 @@ def tile_factoranalysisemloadinggradient_t_kernel(tc, x_bytes, x_scale, p, beta,
         nc.vector.memset(dummy[:], 0.0)
         nc.scalar.activation(out=dummy[:, 1:2], in_=dummy[:, 0:1], func=COPY)
 
-        load(0)
+        xb[0] = keep.tile([P, J * D], U8, name="x_bytes_0", align_bytes=64)
+        for h in range(2):
+            cols = slice(J * D // 2 * h, J * D // 2 * (h + 1))
+            nc.sync.dma_start(out=xb[0][:, cols], in_=xv[0][:, cols])
         xs = keep.tile([P, J], F32, name="xs", align_bytes=64)
         nc.sync.dma_start(out=xs[:], in_=x_scale.rearrange("o (p t) -> p (o t)", t=J))
         load(1)
@@ -176,7 +180,7 @@ def tile_factoranalysisemloadinggradient_t_kernel(tc, x_bytes, x_scale, p, beta,
 
         def drain(i, ci):
             kind, col = CHUNKS[ci]
-            if ci == 0:
+            if i not in zi:
                 zi[i] = work.tile([P, K, J], BF16, name="zi", tag="zi", bufs=2, align_bytes=64)
                 ei[i] = work.tile([P, D, J], BF16, name="ei", tag="ei", bufs=2, align_bytes=64)
             dst = (zi[i] if kind == "z" else ei[i])[:, col:col + P, :]
@@ -194,32 +198,51 @@ def tile_factoranalysisemloadinggradient_t_kernel(tc, x_bytes, x_scale, p, beta,
                 nc.vector.tensor_tensor(out=dst, in0=f, in1=src, op=MULT)
 
         def st2(i):
+            if i >= DIRECT_FROM:
+                if i == DIRECT_FROM:
+                    for j in range(J):
+                        tag = ("acc0", "acc1", "xwords0", "xwords1")[j]
+                        dacc.append(psum.tile([P, K], F32, name=f"dacc{j}", tag=tag, bufs=1))
+                for j in range(J):
+                    nc.tensor.matmul_mx(
+                        out=dacc[j][:],
+                        lhsT=eq[i][0][:, P * j:P * (j + 1)].bitcast(FP8X4), lhsT_scale=eq[i][1][:, P * j:P * (j + 1)],
+                        rhs=zq[i][0][:].bitcast(FP8X4), rhs_scale=zq[i][1][:],
+                        start=(i == DIRECT_FROM), stop=(i == GROUPS - 1))
+                return
             for h in range(2):
                 nc.tensor.matmul_mx(
                     out=acc[h][:],
                     lhsT=zq[i][0][:, P * h:P * (h + 1)].bitcast(FP8X4), lhsT_scale=zq[i][1][:, P * h:P * (h + 1)],
                     rhs=eq[i][0][:].bitcast(FP8X4), rhs_scale=eq[i][1][:],
-                    start=(i == 0), stop=(i == GROUPS - 1))
+                    start=(i == 0), stop=(i == DIRECT_FROM - 1))
 
+        dacc = []
+        ob = []
         acc = [psum.tile([P, 512], F32, name=f"acc{h}", tag=f"acc{h}", bufs=1) for h in range(2)]
 
-        cast(0, 0, "v")
+        xw[0] = work.tile([P, J * D], BF16, name="xw", tag="xw", bufs=3, align_bytes=64)
+        for j in range(2):
+            cols = slice(D * j, D * (j + 1))
+            nc.vector.tensor_copy(out=xw[0][:, cols], in_=xb[0][:, cols].bitcast(FP8))
         cast(0, 1)
         cast(1, 0, "v")
         cast(1, 1, "v")
         transp(0, by_half=True)
-        transp(1)
         rtp = psum.tile([P, 5, P], BF16, name="rtp", tag="ez", bufs=4)
         for j in range(J):
             nc.tensor.transpose(rtp[:, j, :], rows[:, j:GROUP:J], ident_b[:])
         nc.tensor.transpose(rtp[:, 4, :], psi_rows[:], ident_b[:])
+        transp(1)
 
         beta_i = keep.tile([P, K, J], BF16, name="beta_i", align_bytes=64)
-        nc.scalar.copy(out=beta_i[:], in_=beta_raw[:].rearrange("p t n -> p n t"))
+        nc.gpsimd.tensor_scalar(out=beta_i[:], in0=beta_raw[:].rearrange("p t n -> p n t"), scalar1=1.0, scalar2=0.0, op0=MULT, op1=ADD)
         p_i = keep.tile([P, D, J], BF16, name="p_i", align_bytes=64)
         for h in range(4):
             cols = slice(P * h, P * (h + 1))
             src = p_raw[:, :, cols].rearrange("p t n -> p n t")
+            if h == 3:
+                continue
             if h < 2:
                 nc.scalar.copy(out=p_i[:, cols, :], in_=src)
             else:
@@ -229,6 +252,7 @@ def tile_factoranalysisemloadinggradient_t_kernel(tc, x_bytes, x_scale, p, beta,
         nc.vector.tensor_copy(out=rt[:], in_=rtp[:, 0:4, 0:2 * GROUPS].rearrange("p j c -> p c j"))
         psi_c = keep.tile([P, J], F32, name="psi_c", align_bytes=64)
         nc.vector.tensor_copy(out=psi_c[:], in_=rtp[:, 4, 0:J])
+        nc.vector.tensor_copy(out=p_i[:, 384:512, :], in_=p_raw[:, :, 384:512].rearrange("p t n -> p n t"))
         qx(0, 0)
         beta_q = quant(beta_i[:], K, "beta", 1)
         sexit(1)
@@ -237,12 +261,15 @@ def tile_factoranalysisemloadinggradient_t_kernel(tc, x_bytes, x_scale, p, beta,
         cast(3, 0)
         inv = keep.tile([P, J], F32, name="inv", align_bytes=64)
         nc.vector.reciprocal(out=inv[:], in_=psi_c[:])
-        p_q = quant(p_i[:], D, "p", 1)
         qx(0, 1)
+        p_q = quant(p_i[:], D, "p", 1)
         inv_n = keep.tile([P, J], F32, name="inv_n", align_bytes=64)
         nc.vector.tensor_scalar(out=inv_n[:], in0=inv[:], scalar1=1.0 / N, scalar2=None, op0=MULT)
 
         vp = keep.tile([P, J, K], F32, name="vp", align_bytes=64)
+        w = keep.tile([P, J, K], F32, name="w", align_bytes=64)
+        w2 = keep.tile([P, J, K], F32, name="w2", align_bytes=64)
+        ct = keep.tile([P, 2, D], F32, name="ct", align_bytes=64)
         for ci in range(4):
             mm(0, ci)
 
@@ -287,6 +314,8 @@ def tile_factoranalysisemloadinggradient_t_kernel(tc, x_bytes, x_scale, p, beta,
                 h = 0 if tok[2] == "a" else 1
                 if g < GROUPS and (g, h) not in done:
                     cast(g, h)
+            elif tok == "st2p":
+                st2(i - 2)
             elif tok == "st2":
                 if i > 0:
                     st2(i - 1)
@@ -298,11 +327,28 @@ def tile_factoranalysisemloadinggradient_t_kernel(tc, x_bytes, x_scale, p, beta,
                     qx(i + 1, 1)
             elif tok == "qz":
                 zq[i] = quant(zi[i][:], K, "z", 2)
+            elif tok == "qzp":
+                zq[i - 1] = quant(zi[i - 1][:], K, "z", 2)
             elif tok == "qe":
                 eq[i] = quant(ei[i][:], D, "e", 2)
+            elif tok == "kt":
+                for h in range(2):
+                    nc.scalar.copy(out=ct[:, h, :], in_=acc[h][:])
+            elif tok == "wt":
+                for b in range(2):
+                    ob.append(psum.tile([P, 512], F32, name=f"ob{b}", tag=f"xwords{b}", bufs=1))
+                    for jj in range(2):
+                        j = 2 * b + jj
+                        for h in range(2):
+                            nc.tensor.transpose(ob[b][:, K * jj + P * h:K * jj + P * (h + 1)], ct[:, h, P * j:P * (j + 1)], ident_f[:])
+            elif tok == "ws":
+                for j in range(J):
+                    nc.scalar.activation(out=w[:, j, :], in_=ob[j // 2][:, K * (j % 2):K * (j % 2 + 1)], func=COPY, scale=inv_n[:, j:j + 1])
+            elif tok == "wg":
+                nc.gpsimd.tensor_tensor(out=w2[:], in0=w[:], in1=vp[:], op=SUB)
             elif tok == "vp":
-                if i == GROUPS - 3:
-                    for j in range(J):
+                if 4 <= i < 8:
+                    for j in (i - 4,):
                         nc.scalar.activation(out=vp[:, j, :], in_=v_sb[:, j, :], func=COPY, scale=inv[:, j:j + 1])
 
         for i in range(GROUPS):
@@ -310,13 +356,7 @@ def tile_factoranalysisemloadinggradient_t_kernel(tc, x_bytes, x_scale, p, beta,
                 do(i, tok)
         st2(GROUPS - 1)
 
-        ct = keep.tile([P, 2, D], F32, name="ct", align_bytes=64)
-        nc.vector.tensor_copy(out=ct[:, 0, :], in_=acc[0][:])
-        nc.scalar.copy(out=ct[:, 1, :], in_=acc[1][:])
         res = keep.tile([P, J, K], F32, name="res", align_bytes=64)
         for j in range(J):
-            ob = psum.tile([P, K], F32, name="ob", tag="ez", bufs=4)
-            for h in range(2):
-                nc.tensor.transpose(ob[:, P * h:P * (h + 1)], ct[:, h, P * j:P * (j + 1)], ident_f[:])
-            nc.vector.scalar_tensor_tensor(out=res[:, j, :], in0=ob[:], scalar=inv_n[:, j:j + 1], in1=vp[:, j, :], op0=MULT, op1=SUB)
+            nc.vector.scalar_tensor_tensor(out=res[:, j, :], in0=dacc[j][:], scalar=inv_n[:, j:j + 1], in1=w2[:, j, :], op0=MULT, op1=ADD)
             nc.sync.dma_start(out=out[P * j:P * (j + 1), :], in_=res[:, j, :])

from contextlib import ExitStack

import concourse.mybir as mybir
from concourse.masks import make_identity

N, D, K = 8192, 512, 256
P = 128
J = 4
GROUP = P * J
GROUPS = N // GROUP
FLOPS = 2 * N * D * (D + K) + 2 * N * D * K

F32 = mybir.dt.float32
BF16 = mybir.dt.bfloat16
U32 = mybir.dt.uint32
U8 = mybir.dt.uint8
FP8 = mybir.dt.float8_e4m3fn
FP8X4 = mybir.dt.float8_e4m3fn_x4
MULT = mybir.AluOpType.mult
ADD = mybir.AluOpType.add
SUB = mybir.AluOpType.subtract
COPY = mybir.ActivationFunctionType.Copy

Z_ON_SCALAR = (15,)
DIRECT_FROM = 13
GIL_S = ()
SEQ = "g0 g1 gs d0 d1 d2 d3 T0 m4 m5 T1 s01 s23 c3b c4a vp d4 d5 st2 qxa qxb qz M0 M1 M2 M3 qe".split()
SEQ_OF = {0: "g0 g1 gs d0 d1 d2 d3 m4 m5 T0 s01 T1 s23 c3b c4a d4 d5 st2 qxa qxb qz M0 M1 M2 M3 qe".split(), 1: "g0 g1 gs d0 d1 d2 d3 m4 m5 T0 s01 T1 s23 c3b c4a d4 d5 st2 qxa qxb qz M0 M1 M2 M3 qe".split(), 13: "g0 g1 gs d0 d1 d2 d3 T0 m4 m5 T1 s01 s23 c3b c4a d4 d5 st2 kt qxa qxb qz M0 M1 M2 M3 qe".split(), 14: "g0 g1 d0 d1 d2 d3 m4 m5 wt ws d4 d5 qxa qxb qz M0 M1 M2 M3 qe wg".split(), 15: "d0 d1 d2 d3 m4 m5 st2p st2 d4 d5 qz qe".split()}
CHUNKS = [("z", 0), ("z", 128), ("e", 0), ("e", 128), ("e", 256), ("e", 384)]


def tile_factoranalysisemloadinggradient_t_kernel(tc, x_bytes, x_scale, p, beta, r, t, v, psi, out):
    nc = tc.nc
    with ExitStack() as ctx:
        keep = ctx.enter_context(tc.tile_pool(name="keep", bufs=1))
        work = ctx.enter_context(tc.tile_pool(name="work", bufs=2))
        psum = ctx.enter_context(tc.psum_pool(name="psum", bufs=1))
        ctx.enter_context(tc.manual_schedule())

        xb = {}
        xw = {}
        xwords = {}
        xp = {}
        xi = {}
        xc = {}
        banks = {}
        zi = {}
        ei = {}
        zq = {}
        zplanes = {}
        eq = {}

        xv = x_bytes.rearrange("(g m j) k -> g m (j k)", m=P, j=J)

        def load(g):
            xb[g] = keep.tile([P, J * D], U8, name=f"x_bytes_{g}", align_bytes=64)
            nc.sync.dma_start(out=xb[g][:], in_=xv[g])

        rows = keep.tile([P, GROUP], BF16, name="rows", align_bytes=64)
        nc.vector.memset(rows[:], 0.0)
        psi_rows = keep.tile([P, P], BF16, name="psi_rows", align_bytes=64)
        nc.vector.memset(psi_rows[:], 0.0)
        dummy = keep.tile([P, 2], F32, name="dummy")
        nc.vector.memset(dummy[:], 0.0)
        nc.scalar.activation(out=dummy[:, 1:2], in_=dummy[:, 0:1], func=COPY)

        xb[0] = keep.tile([P, J * D], U8, name="x_bytes_0", align_bytes=64)
        for h in range(2):
            cols = slice(J * D // 2 * h, J * D // 2 * (h + 1))
            nc.sync.dma_start(out=xb[0][:, cols], in_=xv[0][:, cols])
        xs = keep.tile([P, J], F32, name="xs", align_bytes=64)
        nc.sync.dma_start(out=xs[:], in_=x_scale.rearrange("o (p t) -> p (o t)", t=J))
        load(1)
        beta_raw = keep.tile([P, J, K], BF16, name="beta_raw", align_bytes=64)
        nc.sync.dma_start(out=beta_raw[:], in_=beta.rearrange("(p t) n -> p t n", t=J))
        p_raw = keep.tile([P, J, D], BF16, name="p_raw", align_bytes=64)
        nc.sync.dma_start(out=p_raw[:], in_=p.rearrange("(p t) n -> p t n", t=J))
        nc.scalar.dma_start(out=rows[0:GROUPS, :], in_=r.rearrange("(g q) -> g q", q=GROUP))
        nc.scalar.dma_start(out=rows[GROUPS:2 * GROUPS, :], in_=t.rearrange("(g q) -> g q", q=GROUP))
        nc.scalar.dma_start(out=psi_rows[0:J, :], in_=psi.rearrange("(j p) -> j p", p=P))
        for g in range(2, 4):
            load(g)
        v_sb = keep.tile([P, J, K], BF16, name="v_sb", align_bytes=64)
        nc.sync.dma_start(out=v_sb[:], in_=v.rearrange("(j p) n -> p j n", p=P))
        for g in range(4, GROUPS):
            load(g)

        ident_f = keep.tile([P, P], F32, name="ident_f", align_bytes=64)
        make_identity(nc, ident_f[:])
        ident_b = keep.tile([P, P], BF16, name="ident_b", align_bytes=64)
        nc.vector.tensor_copy(out=ident_b[:], in_=ident_f[:])

        done = set()

        def cast(g, h, eng=None):
            done.add((g, h))
            if h == 0:
                xw[g] = work.tile([P, J * D], BF16, name="xw", tag="xw", bufs=3, align_bytes=64)
            half = J * D // 2
            cols = slice(h * half, (h + 1) * half)
            src = xb[g][:, cols].bitcast(FP8)
            if eng == "v":
                nc.vector.tensor_copy(out=xw[g][:, cols], in_=src)
            else:
                nc.scalar.copy(out=xw[g][:, cols], in_=src)

        def transp(g, by_half=False, us=(0, 1)):
            words = xw[g][:].bitcast(F32)
            b = xwords.setdefault(g, {})
            for u in us:
                b[u] = psum.tile([P, 512], F32, name=f"xwords{u}", tag="ez" if by_half else f"xwords{u}", bufs=4 if by_half else 1)
            order = [(u, j) for j in range(J) for u in us] if by_half else [(u, j) for u in us for j in range(J)]
            for u, j in order:
                src = words[:, 256 * j + u:256 * (j + 1):2]
                if by_half:
                    dst = b[j // 2][:, 256 * u + 128 * (j % 2):256 * u + 128 * (j % 2) + 128]
                else:
                    dst = b[u][:, 128 * j:128 * (j + 1)]
                nc.tensor.transpose(dst, src, ident_f[:])

        def new_xi(g):
            xi[g] = work.tile([P, GROUP, J], BF16, name="xi", tag="xi", bufs=1, align_bytes=64)

        def vexit(g):
            new_xi(g)
            for h in range(2):
                src = xwords[g][h][:].bitcast(BF16).rearrange("p (u n e) -> p n u e", u=2, e=2)
                dst = xi[g][:, 256 * h:256 * (h + 1), :].rearrange("p n (u e) -> p n u e", e=2)
                sc = xs[:].rearrange("p (u e) -> p u e", e=2).unsqueeze(1).to_broadcast([P, 256, 2, 2])
                nc.vector.tensor_tensor(out=dst, in0=src, in1=sc, op=MULT)

        def sexit(g, ts=(0, 1, 2, 3)):
            if 0 in ts:
                xp[g] = work.tile([P, J, GROUP], BF16, name="xp", tag="xp", bufs=2, align_bytes=64)
            for tt in ts:
                src = xwords[g][tt // 2][:].bitcast(BF16).rearrange("p (n e) -> p e n", e=2)[:, tt % 2, :]
                nc.scalar.activation(out=xp[g][:, tt, :], in_=src, func=COPY, scale=xs[:, tt:tt + 1])

        def gil(g):
            new_xi(g)
            for h in range(2):
                cols = slice(256 * h, 256 * (h + 1))
                nc.gpsimd.tensor_scalar(
                    out=xi[g][:, cols, :], in0=xp[g][:, :, cols].rearrange("p t n -> p n t"),
                    scalar1=1.0, scalar2=0.0, op0=MULT, op1=ADD)

        def quant(src, width, tag, bufs):
            codes = work.tile([P, width], U32, name=tag + "c", tag=tag + "c", bufs=bufs, align_bytes=64)
            scales = work.tile([P, width], U8, name=tag + "s", tag=tag + "s", bufs=bufs, align_bytes=64)
            nc.vector.quantize_mx(out=codes[:].bitcast(FP8X4), scales=scales[:], in_=src.rearrange("p n j -> p (n j)"))
            return codes, scales

        def qx(g, h):
            if h == 0:
                xc[g] = (work.tile([P, GROUP], U32, name="xcodes", tag="xcodes", bufs=3, align_bytes=64),
                         work.tile([P, GROUP], U8, name="xscales", tag="xscales", bufs=3, align_bytes=64))
            cols = slice(256 * h, 256 * (h + 1))
            nc.vector.quantize_mx(out=xc[g][0][:, cols].bitcast(FP8X4), scales=xc[g][1][:, cols],
                                  in_=xi[g][:, cols, :].rearrange("p n j -> p (n j)"))

        def mm(i, ci):
            kind, col = CHUNKS[ci]
            bank = psum.tile([P, 512], F32, name="ez", tag="ez", bufs=4)
            banks[i, ci] = bank
            if kind == "z" and i in Z_ON_SCALAR:
                for jj in range(2):
                    j = 2 * ci + jj
                    nc.tensor.matmul_mx(
                        out=bank[:, K * jj:K * (jj + 1)],
                        lhsT=xc[i][0][:, P * j:P * (j + 1)].bitcast(FP8X4), lhsT_scale=xc[i][1][:, P * j:P * (j + 1)],
                        rhs=beta_q[0][:].bitcast(FP8X4), rhs_scale=beta_q[1][:], start=True, stop=True)
                return
            wc, wsc = (beta_q if kind == "z" else p_q)
            for j in range(J):
                nc.tensor.matmul_mx(
                    out=bank[:, P * j:P * (j + 1)],
                    lhsT=xc[i][0][:, P * j:P * (j + 1)].bitcast(FP8X4), lhsT_scale=xc[i][1][:, P * j:P * (j + 1)],
                    rhs=wc[:, col:col + P].bitcast(FP8X4), rhs_scale=wsc[:, col:col + P],
                    start=True, stop=True)

        def drain(i, ci):
            kind, col = CHUNKS[ci]
            if i not in zi:
                zi[i] = work.tile([P, K, J], BF16, name="zi", tag="zi", bufs=2, align_bytes=64)
                ei[i] = work.tile([P, D, J], BF16, name="ei", tag="ei", bufs=2, align_bytes=64)
            dst = (zi[i] if kind == "z" else ei[i])[:, col:col + P, :]
            f = rt[:, (GROUPS + i if kind == "z" else i), :].unsqueeze(1).to_broadcast([P, P, J])
            src = banks[i, ci][:].rearrange("p (j n) -> p n j", j=J)
            if kind == "z" and i in Z_ON_SCALAR:
                if ci == 0:
                    zplanes[i] = work.tile([P, J, K], BF16, name="zplanes", tag="zplanes", bufs=2, align_bytes=64)
                for jj in range(2):
                    j = 2 * ci + jj
                    nc.scalar.activation(out=zplanes[i][:, j, :], in_=banks[i, ci][:, K * jj:K * (jj + 1)], func=COPY, scale=rt[:, GROUPS + i, j:j + 1])
                if ci == 1:
                    nc.scalar.copy(out=zi[i][:], in_=zplanes[i][:].rearrange("p j n -> p n j"))
            else:
                nc.vector.tensor_tensor(out=dst, in0=f, in1=src, op=MULT)

        def st2(i):
            if i >= DIRECT_FROM:
                if i == DIRECT_FROM:
                    for j in range(J):
                        tag = ("acc0", "acc1", "xwords0", "xwords1")[j]
                        dacc.append(psum.tile([P, K], F32, name=f"dacc{j}", tag=tag, bufs=1))
                for j in range(J):
                    nc.tensor.matmul_mx(
                        out=dacc[j][:],
                        lhsT=eq[i][0][:, P * j:P * (j + 1)].bitcast(FP8X4), lhsT_scale=eq[i][1][:, P * j:P * (j + 1)],
                        rhs=zq[i][0][:].bitcast(FP8X4), rhs_scale=zq[i][1][:],
                        start=(i == DIRECT_FROM), stop=(i == GROUPS - 1))
                return
            for h in range(2):
                nc.tensor.matmul_mx(
                    out=acc[h][:],
                    lhsT=zq[i][0][:, P * h:P * (h + 1)].bitcast(FP8X4), lhsT_scale=zq[i][1][:, P * h:P * (h + 1)],
                    rhs=eq[i][0][:].bitcast(FP8X4), rhs_scale=eq[i][1][:],
                    start=(i == 0), stop=(i == DIRECT_FROM - 1))

        dacc = []
        ob = []
        acc = [psum.tile([P, 512], F32, name=f"acc{h}", tag=f"acc{h}", bufs=1) for h in range(2)]

        xw[0] = work.tile([P, J * D], BF16, name="xw", tag="xw", bufs=3, align_bytes=64)
        for j in range(2):
            cols = slice(D * j, D * (j + 1))
            nc.vector.tensor_copy(out=xw[0][:, cols], in_=xb[0][:, cols].bitcast(FP8))
        cast(0, 1)
        cast(1, 0, "v")
        cast(1, 1, "v")
        transp(0, by_half=True)
        rtp = psum.tile([P, 5, P], BF16, name="rtp", tag="ez", bufs=4)
        for j in range(J):
            nc.tensor.transpose(rtp[:, j, :], rows[:, j:GROUP:J], ident_b[:])
        nc.tensor.transpose(rtp[:, 4, :], psi_rows[:], ident_b[:])
        transp(1)

        beta_i = keep.tile([P, K, J], BF16, name="beta_i", align_bytes=64)
        nc.gpsimd.tensor_scalar(out=beta_i[:], in0=beta_raw[:].rearrange("p t n -> p n t"), scalar1=1.0, scalar2=0.0, op0=MULT, op1=ADD)
        p_i = keep.tile([P, D, J], BF16, name="p_i", align_bytes=64)
        for h in range(4):
            cols = slice(P * h, P * (h + 1))
            src = p_raw[:, :, cols].rearrange("p t n -> p n t")
            if h == 3:
                continue
            if h < 2:
                nc.scalar.copy(out=p_i[:, cols, :], in_=src)
            else:
                nc.gpsimd.tensor_scalar(out=p_i[:, cols, :], in0=src, scalar1=1.0, scalar2=0.0, op0=MULT, op1=ADD)
        vexit(0)
        rt = keep.tile([P, 2 * GROUPS, J], F32, name="rt", align_bytes=64)
        nc.vector.tensor_copy(out=rt[:], in_=rtp[:, 0:4, 0:2 * GROUPS].rearrange("p j c -> p c j"))
        psi_c = keep.tile([P, J], F32, name="psi_c", align_bytes=64)
        nc.vector.tensor_copy(out=psi_c[:], in_=rtp[:, 4, 0:J])
        nc.vector.tensor_copy(out=p_i[:, 384:512, :], in_=p_raw[:, :, 384:512].rearrange("p t n -> p n t"))
        qx(0, 0)
        beta_q = quant(beta_i[:], K, "beta", 1)
        sexit(1)
        cast(2, 0)
        cast(2, 1)
        cast(3, 0)
        inv = keep.tile([P, J], F32, name="inv", align_bytes=64)
        nc.vector.reciprocal(out=inv[:], in_=psi_c[:])
        qx(0, 1)
        p_q = quant(p_i[:], D, "p", 1)
        inv_n = keep.tile([P, J], F32, name="inv_n", align_bytes=64)
        nc.vector.tensor_scalar(out=inv_n[:], in0=inv[:], scalar1=1.0 / N, scalar2=None, op0=MULT)

        vp = keep.tile([P, J, K], F32, name="vp", align_bytes=64)
        w = keep.tile([P, J, K], F32, name="w", align_bytes=64)
        w2 = keep.tile([P, J, K], F32, name="w2", align_bytes=64)
        ct = keep.tile([P, 2, D], F32, name="ct", align_bytes=64)
        for ci in range(4):
            mm(0, ci)

        def gil_half(g, h, eng):
            if h == 0:
                new_xi(g)
            cols = slice(256 * h, 256 * (h + 1))
            src = xp[g][:, :, cols].rearrange("p t n -> p n t")
            if eng == "s":
                nc.scalar.copy(out=xi[g][:, cols, :], in_=src)
            else:
                nc.gpsimd.tensor_scalar(out=xi[g][:, cols, :], in0=src, scalar1=1.0, scalar2=0.0, op0=MULT, op1=ADD)

        def do(i, tok):
            if tok == "g0":
                if i + 1 < GROUPS:
                    gil_half(i + 1, 0, "g")
            elif tok == "g1":
                if i + 1 < GROUPS and i + 1 not in GIL_S:
                    gil_half(i + 1, 1, "g")
            elif tok == "gs":
                if i + 1 < GROUPS and i + 1 in GIL_S:
                    gil_half(i + 1, 1, "s")
            elif tok[0] == "d":
                drain(i, int(tok[1]))
            elif tok[0] == "m":
                mm(i, int(tok[1]))
            elif tok[0] == "M":
                if i + 1 < GROUPS:
                    mm(i + 1, int(tok[1]))
            elif tok[0] == "T":
                if i + 2 < GROUPS:
                    transp(i + 2, us=(int(tok[1]),))
            elif tok == "s01":
                if i + 2 < GROUPS:
                    sexit(i + 2, (0, 1))
            elif tok == "s23":
                if i + 2 < GROUPS:
                    sexit(i + 2, (2, 3))
            elif tok[0] == "c":
                g = i + int(tok[1])
                h = 0 if tok[2] == "a" else 1
                if g < GROUPS and (g, h) not in done:
                    cast(g, h)
            elif tok == "st2p":
                st2(i - 2)
            elif tok == "st2":
                if i > 0:
                    st2(i - 1)
            elif tok == "qxa":
                if i + 1 < GROUPS:
                    qx(i + 1, 0)
            elif tok == "qxb":
                if i + 1 < GROUPS:
                    qx(i + 1, 1)
            elif tok == "qz":
                zq[i] = quant(zi[i][:], K, "z", 2)
            elif tok == "qzp":
                zq[i - 1] = quant(zi[i - 1][:], K, "z", 2)
            elif tok == "qe":
                eq[i] = quant(ei[i][:], D, "e", 2)
            elif tok == "kt":
                for h in range(2):
                    nc.scalar.copy(out=ct[:, h, :], in_=acc[h][:])
            elif tok == "wt":
                for b in range(2):
                    ob.append(psum.tile([P, 512], F32, name=f"ob{b}", tag=f"xwords{b}", bufs=1))
                    for jj in range(2):
                        j = 2 * b + jj
                        for h in range(2):
                            nc.tensor.transpose(ob[b][:, K * jj + P * h:K * jj + P * (h + 1)], ct[:, h, P * j:P * (j + 1)], ident_f[:])
            elif tok == "ws":
                for j in range(J):
                    nc.scalar.activation(out=w[:, j, :], in_=ob[j // 2][:, K * (j % 2):K * (j % 2 + 1)], func=COPY, scale=inv_n[:, j:j + 1])
            elif tok == "wg":
                nc.gpsimd.tensor_tensor(out=w2[:], in0=w[:], in1=vp[:], op=SUB)
            elif tok == "vp":
                if 4 <= i < 8:
                    for j in (i - 4,):
                        nc.scalar.activation(out=vp[:, j, :], in_=v_sb[:, j, :], func=COPY, scale=inv[:, j:j + 1])

        for i in range(GROUPS):
            for tok in SEQ_OF.get(i, SEQ):
                do(i, tok)
        st2(GROUPS - 1)

        res = keep.tile([P, J, K], F32, name="res", align_bytes=64)
        for j in range(J):
            nc.vector.scalar_tensor_tensor(out=res[:, j, :], in0=dacc[j][:], scalar=inv_n[:, j:j + 1], in1=w2[:, j, :], op0=MULT, op1=ADD)
            nc.sync.dma_start(out=out[P * j:P * (j + 1), :], in_=res[:, j, :])
